import numpy as np
import ml_dtypes


def mxq(x, axis, fmt="e4m3"):
    dtype, down = {"e4m3": (ml_dtypes.float8_e4m3fn, 7), "e5m2": (ml_dtypes.float8_e5m2, 14)}[fmt]
    v = np.moveaxis(np.asarray(x, np.float32).astype(ml_dtypes.bfloat16).astype(np.float64), axis, -1)
    blocks = v.reshape(v.shape[:-1] + (-1, 32))
    amax = np.abs(blocks).max(-1, keepdims=True)
    byte = np.maximum(np.where(amax > 0, np.frexp(amax)[1] - 1 + 127, 0) - down, 1)
    scale = np.exp2(byte - 127.0)
    codes = (blocks / scale).astype(np.float32).astype(dtype).astype(np.float64)
    return np.moveaxis((codes * scale).reshape(v.shape), -1, axis)


WIDE = False


def mx_kscale(k):
    if not WIDE:
        return np.ones(k)
    levels = np.array([10, -10, 5, -5, 0])
    if k % 512:
        return np.exp2(np.random.permutation(np.resize(levels, k // 32))).repeat(32)
    a = np.empty((k // 512, 16))
    for p in range(k // 512):
        a[p, :8] = np.random.permutation(np.resize(levels, 8))
        for g in range(8):
            far = levels[np.abs(levels - a[p, g]) >= 10]
            a[p, g + 8] = far[np.random.randint(len(far))]
    return np.exp2(a.ravel()).repeat(32)


BF16 = ml_dtypes.bfloat16


def bf(x):
    return np.asarray(x, np.float32).astype(BF16)


def f64(x):
    return np.asarray(x).astype(np.float64)


E2M1 = np.array([0.0, 0.5, 1.0, 1.5, 2.0, 3.0, 4.0, 6.0, -0.0, -0.5, -1.0, -1.5, -2.0, -3.0, -4.0, -6.0])


def pack_weight(w, fmt):
    k, n = w.shape
    w = f64(bf(w)).reshape(k // 32, 32, n)
    amax = np.abs(w).max(1)
    if fmt == "e4m3":
        byte = np.frexp(amax)[1] - 1 + 127 - 7
    else:
        mant, ex = np.frexp(amax / 6.0)
        byte = np.where(mant > 0.5, ex, ex - 1) + 127
    byte = np.clip(np.where(amax > 0, byte, 1), 1, 254)
    scaled = (w * np.exp2(127.0 - byte)[:, None, :]).reshape(k, n).astype(np.float32)
    by_word = np.ascontiguousarray(scaled.reshape(k // 512, 128, 4, n).transpose(0, 1, 3, 2))
    if fmt == "e4m3":
        words = by_word.astype(ml_dtypes.float8_e4m3fn).view(np.uint8)
    else:
        c = by_word.astype(ml_dtypes.float4_e2m1fn).view(np.uint8) & 0xF
        words = c[..., 0::2] | (c[..., 1::2] << 4)
    return np.ascontiguousarray(words), np.ascontiguousarray(byte.astype(np.uint8).reshape(k // 512, 16, n))


def unpack_weight(words, scales, fmt):
    g, p, n, _ = words.shape
    if fmt == "e4m3":
        vals = np.ascontiguousarray(words).view(ml_dtypes.float8_e4m3fn).astype(np.float64)
    else:
        nib = np.empty((g, p, n, 4), np.uint8)
        nib[..., 0::2] = words & 0xF
        nib[..., 1::2] = words >> 4
        vals = E2M1[nib]
    vals = vals * np.repeat(np.exp2(scales.astype(np.float64) - 127.0), 8, axis=1)[..., None]
    return vals.transpose(0, 1, 3, 2).reshape(g * 512, n)
def pack4(w):
    words, scales = pack_weight(w, "e2m1")
    return words.reshape(words.shape[0], 128, -1), scales


def unpack4(words, scales):
    return unpack_weight(words.reshape(words.shape[0], 128, -1, 2), scales, "e2m1")


P, K, F, D, L, C = 512, 1024, 1024, 1024, 8, 128


def draw0():
    s = mx_kscale(K)
    u = mx_kscale(D)
    t = mx_kscale(F)
    wkv = np.random.standard_normal((D, 2 * L * C)) / np.sqrt(D) / u[:, None]
    wkv_words, wkv_scales = pack4(wkv)
    return {
        "codes": bf(np.random.standard_normal((P, K)) * s),
        "w_in": bf(np.random.standard_normal((K, F)) / np.sqrt(K) / s[:, None]),
        "bias": bf(0.3 * np.random.standard_normal(F)),
        "gain": bf((1 + 0.1 * np.random.standard_normal(F)) * t),
        "w_up": bf(np.random.standard_normal((F, D)) / np.sqrt(np.sqrt(F)) * u / t[:, None]),
        "wkv_words": wkv_words,
        "wkv_scales": wkv_scales,
    }


def core(codes, w_in, bias, gain, w_up, wkv_words, wkv_scales):
    a = mxq(f64(codes), 1, "e4m3") @ mxq(f64(w_in), 0, "e4m3")
    h = np.tanh(a + f64(bias)) * f64(gain)
    w = unpack4(wkv_words, wkv_scales)
    m = mxq(f64(w_up), 1, "e4m3") @ w
    y = mxq(h, 1, "e4m3") @ mxq(m, 0, "e4m3")
    keys = y[:, :L * C]
    values = y[:, L * C:]
    return keys, values


def e4m3fn_bytes(y):
    return np.clip(np.asarray(y, np.float64), -448.0, 448.0).astype(np.float32).astype(ml_dtypes.float8_e4m3fn).view(np.uint8)


def e4m3fn_values(b):
    return np.asarray(b, np.uint8).view(ml_dtypes.float8_e4m3fn).astype(np.float64)


def setup_inputs():
    d = draw0()
    x0 = np.asarray(d['w_in']).astype(np.float64)
    s = (np.max(np.abs(x0), axis=(1,), keepdims=True) / 448.0).astype(np.float32)
    out = {}
    for k, v in d.items():
        if k == 'w_in':
            out['w_in_bytes'] = e4m3fn_bytes(x0 / s.astype(np.float64))
            out['w_in_scale'] = s
        else:
            out[k] = v
    return out


def reference(codes, w_in_bytes, w_in_scale, bias, gain, w_up, wkv_words, wkv_scales):
    return core(codes, e4m3fn_values(w_in_bytes) * w_in_scale.astype(np.float64), bias, gain, w_up, wkv_words, wkv_scales)

@@ -1,0 +1,318 @@
+from contextlib import ExitStack
+
+import concourse.mybir as mybir
+from concourse.masks import make_identity
+
+P = 128
+ROWS, K, F, D, N = 512, 1024, 1024, 1024, 2048
+FLOPS = 2 * (ROWS * K * F + F * D * N + ROWS * F * N)
+
+F32 = mybir.dt.float32
+BF16 = mybir.dt.bfloat16
+I32 = mybir.dt.int32
+U32 = mybir.dt.uint32
+U8 = mybir.dt.uint8
+FP8 = mybir.dt.float8_e4m3fn
+FP8X4 = mybir.dt.float8_e4m3fn_x4
+FP4X4 = mybir.dt.float4_e2m1fn_x4
+MULT = mybir.AluOpType.mult
+TANH = mybir.ActivationFunctionType.Tanh
+
+
+def tile_prefix_tuning_kv_s11_kernel(
+    tc, codes, w_in_bytes, w_in_scale, bias, gain, w_up, wkv_words, wkv_scales, keys, values
+):
+    nc = tc.nc
+    with ExitStack() as ctx:
+        keep = ctx.enter_context(tc.tile_pool(name="keep", bufs=1))
+        wst = ctx.enter_context(tc.tile_pool(name="wst", bufs=3))
+        mst = ctx.enter_context(tc.tile_pool(name="mst", bufs=16))
+        yst = ctx.enter_context(tc.tile_pool(name="yst", bufs=8))
+        psum = ctx.enter_context(tc.psum_pool(name="psum", bufs=8))
+
+        ident = keep.tile([P, P], F32, name="ident")
+        make_identity(nc, ident[:])
+
+        wu_raw = [keep.tile([P, 4, D], BF16, name="wu_raw%d" % g, align_bytes=64) for g in range(2)]
+        wuq = [keep.tile([P, 4, 256], U32, name="wuq%d" % g, align_bytes=64) for g in range(2)]
+        wus = [keep.tile([P, 4, 256], U8, name="wus%d" % g, align_bytes=64) for g in range(2)]
+        w4 = keep.tile([P, 2, 2 * N], U8, name="w4", align_bytes=64)
+        w4s = keep.tile([P, 2, N], U8, name="w4s", align_bytes=64)
+        craw = keep.tile([P, 4, K], BF16, name="craw", align_bytes=64)
+        cg = keep.tile([P, 2, ROWS, 4], BF16, name="cg", align_bytes=64)
+        cq = keep.tile([P, 2, ROWS], U32, name="cq", align_bytes=64)
+        cs = keep.tile([P, 2, ROWS], U8, name="cs", align_bytes=64)
+        wi = keep.tile([P, 2, 4, F], U8, name="wi", align_bytes=64)
+        wisc = keep.tile([P, 2, 4], F32, name="wisc")
+        wb = keep.tile([P, 2, 4, F], BF16, name="wb", align_bytes=64)
+        wg = keep.tile([P, 2, 2, 2048], BF16, name="wg", align_bytes=64)
+        wq = keep.tile([P, 2, 2, 512], U32, name="wq", align_bytes=64)
+        ws = keep.tile([P, 2, 2, 512], U8, name="ws", align_bytes=64)
+        bcol = keep.tile([P, 2, 4], BF16, name="bcol")
+        gcol = keep.tile([P, 2, 4], BF16, name="gcol")
+        th = [keep.tile([P, 4, ROWS], F32, name="th%d" % g, align_bytes=64) for g in range(2)]
+        hg = [keep.tile([P, ROWS, 4], BF16, name="hg%d" % g, align_bytes=64) for g in range(2)]
+        hq = [keep.tile([P, ROWS], U32, name="hq%d" % g, align_bytes=64) for g in range(2)]
+        hs = [keep.tile([P, ROWS], U8, name="hs%d" % g, align_bytes=64) for g in range(2)]
+        mq = [keep.tile([P, N], U32, name="mq%d" % g, align_bytes=64) for g in range(2)]
+        ms = [keep.tile([P, N], U8, name="ms%d" % g, align_bytes=64) for g in range(2)]
+        warm = keep.tile([P, 2], F32, name="warm")
+
+        ctx.enter_context(tc.manual_schedule())
+
+        nc.vector.memset(w4s[:, :, 0:512].bitcast(I32), 0)
+        nc.vector.memset(w4s[:, :, 512:N].bitcast(I32), 0)
+        nc.vector.memset(warm[:], 0.0)
+        nc.scalar.activation(out=warm[:, 1:2], in_=warm[:, 0:1], func=TANH)
+
+        wu_src = w_up.rearrange("(g p t) d -> g p t d", p=P, t=4)
+
+        def load_wu(g, t0, t1):
+            nc.sync.dma_start(out=wu_raw[g][:, t0:t1, :], in_=wu_src[g][:, t0:t1, :])
+
+        def load_w4(n0, n1):
+            nc.sync.dma_start(
+                out=w4[:, :, 2 * n0 : 2 * n1].bitcast(I32),
+                in_=wkv_words.rearrange("g p b -> p g b")[:, :, 2 * n0 : 2 * n1].bitcast(I32),
+            )
+
+        def load_w4s(n0, n1):
+            for q in range(4):
+                nc.sync.dma_start(
+                    out=w4s[32 * q : 32 * q + 4, :, n0:n1].bitcast(I32),
+                    in_=wkv_scales[:, 4 * q : 4 * q + 4, n0:n1].rearrange("g r n -> r g n").bitcast(I32),
+                )
+
+        load_wu(0, 0, 1)
+        load_w4s(0, 512)
+        load_wu(0, 1, 2)
+        load_wu(0, 2, 4)
+        load_w4(0, 512)
+        load_w4(512, 1024)
+        load_w4s(512, N)
+        load_w4(1024, N)
+        wi_src = w_in_bytes.rearrange("(g p t) f -> g p t f", p=P, t=4)
+        nc.gpsimd.dma_start(out=wisc[:], in_=w_in_scale.rearrange("(g p t) o -> p g (t o)", p=P, t=4))
+        nc.gpsimd.dma_start(out=bcol[:], in_=bias.rearrange("(g p t) -> p g t", p=P, t=4))
+        nc.gpsimd.dma_start(out=gcol[:], in_=gain.rearrange("(g p t) -> p g t", p=P, t=4))
+        for g in range(2):
+            nc.sync.dma_start(out=wi[:, g], in_=wi_src[g])
+        c_src = codes.rearrange("(r p) k -> p r k", p=P)
+        for h in range(2):
+            nc.sync.dma_start(out=craw[:, 2 * h : 2 * h + 2, :], in_=c_src[:, 2 * h : 2 * h + 2, :])
+        load_wu(1, 0, 2)
+        load_wu(1, 2, 4)
+
+        def copy_out(eng, out, in_):
+            if eng == "S":
+                nc.scalar.copy(out=out, in_=in_)
+            else:
+                nc.vector.tensor_copy(out=out, in_=in_)
+
+        def bank():
+            b = psum.tile([P, 512], F32, name="bank", tag="bank")
+            return b
+
+        def turn(words):
+            b = bank()
+            for a in range(2):
+                for u in range(2):
+                    i = 2 * a + u
+                    nc.tensor.transpose(
+                        b[:, 128 * i : 128 * i + 128],
+                        words[:, 256 * a + u : 256 * (a + 1) : 2],
+                        ident[:],
+                    )
+            return b
+
+        def turn_wu(g, t, eng):
+            b = turn(wu_raw[g][:, t, :].bitcast(F32))
+            x = wst.tile([P, 2, 128, 4], BF16, name="wux", tag="wux", align_bytes=64)
+            copy_out(eng, x[:].bitcast(F32), b[:].rearrange("p (a u r) -> p a r u", a=2, u=2))
+            return x
+
+        def quant_wu(g, t, x):
+            nc.vector.quantize_mx(
+                out=wuq[g][:, t, :].bitcast(FP8X4),
+                scales=wus[g][:, t, :],
+                in_=x[:].rearrange("p a r j -> p (a r j)"),
+            )
+
+        def turn_c(r, eng):
+            b = turn(craw[:, r, :].bitcast(F32))
+            copy_out(
+                eng,
+                cg[:, :, 128 * r : 128 * r + 128, :].bitcast(F32),
+                b[:].rearrange("p (a u r) -> p a r u", a=2, u=2),
+            )
+
+        def quant_c(g):
+            nc.vector.quantize_mx(
+                out=cq[:, g, :].bitcast(FP8X4), scales=cs[:, g, :], in_=cg[:, g].rearrange("p n j -> p (n j)")
+            )
+
+        def widen(g, t):
+            nc.vector.tensor_scalar(
+                out=wb[:, g, t, :],
+                in0=wi[:, g, t, :].bitcast(FP8),
+                scalar1=wisc[:, g, t : t + 1],
+                scalar2=None,
+                op0=MULT,
+            )
+
+        def lace(g, h):
+            nc.vector.tensor_copy(
+                out=wg[:, g, h, :].rearrange("p (t m j) -> p t m j", t=4, j=4),
+                in_=wb[:, g, :, 512 * h : 512 * h + 512].rearrange("p j (m t) -> p t m j", t=4),
+            )
+
+        def quant_wi(g, h):
+            nc.vector.quantize_mx(
+                out=wq[:, g, h, :].bitcast(FP8X4), scales=ws[:, g, h, :], in_=wg[:, g, h, :]
+            )
+
+        mx_tiles = {}
+
+        def unit(g, c, eng):
+            b = bank()
+            for t in range(4):
+                for a in range(2):
+                    nc.tensor.matmul_mx(
+                        out=b[:, 128 * t : 128 * t + 128],
+                        lhsT=wuq[g][:, t, 128 * a : 128 * a + 128].bitcast(FP8X4),
+                        lhsT_scale=wus[g][:, t, 128 * a : 128 * a + 128],
+                        rhs=w4[:, a, 256 * c : 256 * c + 256].bitcast(FP4X4),
+                        rhs_scale=w4s[:, a, 128 * c : 128 * c + 128],
+                        start=(a == 0),
+                        stop=(a == 1),
+                    )
+            if c % 2 == 0:
+                x = mst.tile([P, 2, 128, 4], BF16, name="mx", tag="mx", align_bytes=64)
+                mx_tiles[(g, c // 2)] = x
+            x = mx_tiles[(g, c // 2)]
+            copy_out(eng, x[:, c % 2], b[:].rearrange("p (t n) -> p n t", t=4))
+
+        def quant_m(g, d):
+            x = mx_tiles[(g, d)]
+            nc.vector.quantize_mx(
+                out=mq[g][:, 256 * d : 256 * d + 256].bitcast(FP8X4),
+                scales=ms[g][:, 256 * d : 256 * d + 256],
+                in_=x[:].rearrange("p i n j -> p (i n j)"),
+            )
+
+        def hidden(h, t):
+            b = bank()
+            for g in range(2):
+                nc.tensor.matmul_mx(
+                    out=b[:],
+                    lhsT=wq[:, g, h, 128 * t : 128 * t + 128].bitcast(FP8X4),
+                    lhsT_scale=ws[:, g, h, 128 * t : 128 * t + 128],
+                    rhs=cq[:, g, :].bitcast(FP8X4),
+                    rhs_scale=cs[:, g, :],
+                    start=(g == 0),
+                    stop=(g == 1),
+                )
+            nc.scalar.activation(out=th[h][:, t, :], in_=b[:], func=TANH, bias=bcol[:, h, t : t + 1])
+
+        def gains(h):
+            nc.vector.tensor_tensor(
+                out=hg[h][:],
+                in0=th[h][:].rearrange("p t n -> p n t"),
+                in1=gcol[:, h, :].unsqueeze(1).to_broadcast([P, ROWS, 4]),
+                op=MULT,
+            )
+
+        def quant_h(h):
+            nc.vector.quantize_mx(
+                out=hq[h][:].bitcast(FP8X4), scales=hs[h][:], in_=hg[h][:].rearrange("p n j -> p (n j)")
+            )
+
+        def final(i, c, eng):
+            b = bank()
+            for g in range(2):
+                nc.tensor.matmul_mx(
+                    out=b[:],
+                    lhsT=hq[g][:, 128 * i : 128 * i + 128].bitcast(FP8X4),
+                    lhsT_scale=hs[g][:, 128 * i : 128 * i + 128],
+                    rhs=mq[g][:, 512 * c : 512 * c + 512].bitcast(FP8X4),
+                    rhs_scale=ms[g][:, 512 * c : 512 * c + 512],
+                    start=(g == 0),
+                    stop=(g == 1),
+                )
+            y = yst.tile([P, 512], F32, name="y", tag="y", align_bytes=64)
+            copy_out(eng, y[:], b[:])
+            dst = keys if c < 2 else values
+            nc.sync.dma_start(
+                out=dst[128 * i : 128 * i + 128, 512 * (c % 2) : 512 * (c % 2) + 512], in_=y[:]
+            )
+
+        xs = []
+        for t in range(4):
+            xs.append(turn_wu(0, t, "S"))
+            quant_wu(0, t, xs[t])
+        for c in range(0, 4):
+            unit(0, c, "S")
+        quant_m(0, 0)
+        for c in range(4, 8):
+            unit(0, c, "S")
+            widen(0, c - 4)
+        quant_m(0, 1)
+        for r in range(4):
+            turn_c(r, "S")
+            widen(1, r)
+        lace(0, 0)
+        lace(1, 0)
+        for c in range(8, 12):
+            unit(0, c, "S")
+        quant_wi(0, 0)
+        quant_c(0)
+        quant_wi(1, 0)
+        quant_c(1)
+        lace(0, 1)
+        ys = []
+        for t in range(4):
+            ys.append(turn_wu(1, t, "S"))
+            quant_wu(1, t, ys[t])
+        lace(1, 1)
+        quant_wi(0, 1)
+        quant_wi(1, 1)
+        for c in range(12, 16):
+            unit(0, c, "S")
+        for t in range(4):
+            hidden(0, t)
+        for c in range(0, 4):
+            unit(1, c, "S")
+        quant_m(0, 2)
+        quant_m(0, 3)
+        gains(0)
+        for t in range(4):
+            hidden(1, t)
+        quant_m(0, 4)
+        quant_h(0)
+        quant_m(0, 5)
+        quant_m(0, 6)
+        for c in range(4, 8):
+            unit(1, c, "SVSV"[c % 4])
+        quant_m(0, 7)
+        gains(1)
+        quant_m(1, 0)
+        quant_m(1, 1)
+        quant_h(1)
+        for c in range(8, 12):
+            unit(1, c, "S")
+        quant_m(1, 2)
+        quant_m(1, 3)
+        for i in range(4):
+            final(i, 0, "VSVS"[i])
+        quant_m(1, 4)
+        quant_m(1, 5)
+        for c in range(12, 16):
+            unit(1, c, "SVSV"[c % 4])
+        quant_m(1, 6)
+        for i in range(4):
+            final(i, 1, "VSVS"[i])
+        quant_m(1, 7)
+        for i in range(4):
+            final(i, 2, "VSVS"[i])
+        for i in range(4):
+            final(i, 3, "VSVS"[i])

@@ -16,6 +16,7 @@ FP8 = mybir.dt.float8_e4m3fn
 FP8X4 = mybir.dt.float8_e4m3fn_x4
 FP4X4 = mybir.dt.float4_e2m1fn_x4
 MULT = mybir.AluOpType.mult
+COPY = mybir.ActivationFunctionType.Copy
 TANH = mybir.ActivationFunctionType.Tanh
 
 
@@ -25,9 +26,9 @@ def tile_prefix_tuning_kv_s11_kernel(
     nc = tc.nc
     with ExitStack() as ctx:
         keep = ctx.enter_context(tc.tile_pool(name="keep", bufs=1))
-        wst = ctx.enter_context(tc.tile_pool(name="wst", bufs=3))
+        wst = ctx.enter_context(tc.tile_pool(name="wst", bufs=8))
         mst = ctx.enter_context(tc.tile_pool(name="mst", bufs=16))
-        yst = ctx.enter_context(tc.tile_pool(name="yst", bufs=8))
+        yst = ctx.enter_context(tc.tile_pool(name="yst", bufs=16))
         psum = ctx.enter_context(tc.psum_pool(name="psum", bufs=8))
 
         ident = keep.tile([P, P], F32, name="ident")
@@ -86,22 +87,23 @@ def tile_prefix_tuning_kv_s11_kernel(
         load_wu(0, 0, 1)
         load_w4s(0, 512)
         load_wu(0, 1, 2)
-        load_wu(0, 2, 4)
+        load_wu(0, 2, 3)
+        load_wu(0, 3, 4)
         load_w4(0, 512)
+        wi_src = w_in_bytes.rearrange("(g p t) f -> g p t f", p=P, t=4)
+        nc.sync.dma_start(out=wisc[:], in_=w_in_scale.rearrange("(g p t) o -> p g (t o)", p=P, t=4))
+        nc.sync.dma_start(out=wi[:, 0], in_=wi_src[0])
         load_w4(512, 1024)
         load_w4s(512, N)
+        nc.sync.dma_start(out=wi[:, 1], in_=wi_src[1])
         load_w4(1024, N)
-        wi_src = w_in_bytes.rearrange("(g p t) f -> g p t f", p=P, t=4)
-        nc.gpsimd.dma_start(out=wisc[:], in_=w_in_scale.rearrange("(g p t) o -> p g (t o)", p=P, t=4))
-        nc.gpsimd.dma_start(out=bcol[:], in_=bias.rearrange("(g p t) -> p g t", p=P, t=4))
-        nc.gpsimd.dma_start(out=gcol[:], in_=gain.rearrange("(g p t) -> p g t", p=P, t=4))
-        for g in range(2):
-            nc.sync.dma_start(out=wi[:, g], in_=wi_src[g])
         c_src = codes.rearrange("(r p) k -> p r k", p=P)
         for h in range(2):
             nc.sync.dma_start(out=craw[:, 2 * h : 2 * h + 2, :], in_=c_src[:, 2 * h : 2 * h + 2, :])
         load_wu(1, 0, 2)
         load_wu(1, 2, 4)
+        nc.sync.dma_start(out=bcol[:], in_=bias.rearrange("(g p t) -> p g t", p=P, t=4))
+        nc.sync.dma_start(out=gcol[:], in_=gain.rearrange("(g p t) -> p g t", p=P, t=4))
 
         def copy_out(eng, out, in_):
             if eng == "S":
@@ -125,21 +127,23 @@ def tile_prefix_tuning_kv_s11_kernel(
                     )
             return b
 
-        def turn_wu(g, t, eng):
-            b = turn(wu_raw[g][:, t, :].bitcast(F32))
-            x = wst.tile([P, 2, 128, 4], BF16, name="wux", tag="wux", align_bytes=64)
-            copy_out(eng, x[:].bitcast(F32), b[:].rearrange("p (a u r) -> p a r u", a=2, u=2))
-            return x
+        banks = {}
+        wux = {}
 
-        def quant_wu(g, t, x):
+        def drain_wu(g, t, b, eng):
+            x = wst.tile([P, 2, 128, 4], BF16, name="wux", tag="wux", align_bytes=64)
+            wux[(g, t)] = x
+            copy_out(eng, x[:].bitcast(F32), b[:].rearrange("p (a u r) -> p a r u", a=2, u=2))
+
+        def quant_wu(g, t):
+            x = wux[(g, t)]
             nc.vector.quantize_mx(
                 out=wuq[g][:, t, :].bitcast(FP8X4),
                 scales=wus[g][:, t, :],
                 in_=x[:].rearrange("p a r j -> p (a r j)"),
             )
 
-        def turn_c(r, eng):
-            b = turn(craw[:, r, :].bitcast(F32))
+        def drain_c(r, b, eng):
             copy_out(
                 eng,
                 cg[:, :, 128 * r : 128 * r + 128, :].bitcast(F32),
@@ -151,7 +155,12 @@ def tile_prefix_tuning_kv_s11_kernel(
                 out=cq[:, g, :].bitcast(FP8X4), scales=cs[:, g, :], in_=cg[:, g].rearrange("p n j -> p (n j)")
             )
 
-        def widen(g, t):
+        def widen(g, t, eng="V"):
+            if eng == "S":
+                nc.scalar.activation(
+                    out=wb[:, g, t, :], in_=wi[:, g, t, :].bitcast(FP8), func=COPY, scale=wisc[:, g, t : t + 1]
+                )
+                return
             nc.vector.tensor_scalar(
                 out=wb[:, g, t, :],
                 in0=wi[:, g, t, :].bitcast(FP8),
@@ -173,7 +182,7 @@ def tile_prefix_tuning_kv_s11_kernel(
 
         mx_tiles = {}
 
-        def unit(g, c, eng):
+        def unit(g, c):
             b = bank()
             for t in range(4):
                 for a in range(2):
@@ -186,7 +195,10 @@ def tile_prefix_tuning_kv_s11_kernel(
                         start=(a == 0),
                         stop=(a == 1),
                     )
-            if c % 2 == 0:
+            return b
+
+        def drain_m(g, c, b, eng):
+            if (g, c // 2) not in mx_tiles:
                 x = mst.tile([P, 2, 128, 4], BF16, name="mx", tag="mx", align_bytes=64)
                 mx_tiles[(g, c // 2)] = x
             x = mx_tiles[(g, c // 2)]
@@ -212,6 +224,9 @@ def tile_prefix_tuning_kv_s11_kernel(
                     start=(g == 0),
                     stop=(g == 1),
                 )
+            return b
+
+        def drain_h(h, t, b):
             nc.scalar.activation(out=th[h][:, t, :], in_=b[:], func=TANH, bias=bcol[:, h, t : t + 1])
 
         def gains(h):
@@ -227,7 +242,7 @@ def tile_prefix_tuning_kv_s11_kernel(
                 out=hq[h][:].bitcast(FP8X4), scales=hs[h][:], in_=hg[h][:].rearrange("p n j -> p (n j)")
             )
 
-        def final(i, c, eng):
+        def final(i, c):
             b = bank()
             for g in range(2):
                 nc.tensor.matmul_mx(
@@ -239,6 +254,9 @@ def tile_prefix_tuning_kv_s11_kernel(
                     start=(g == 0),
                     stop=(g == 1),
                 )
+            return b
+
+        def drain_y(i, c, b, eng):
             y = yst.tile([P, 512], F32, name="y", tag="y", align_bytes=64)
             copy_out(eng, y[:], b[:])
             dst = keys if c < 2 else values
@@ -246,73 +264,61 @@ def tile_prefix_tuning_kv_s11_kernel(
                 out=dst[128 * i : 128 * i + 128, 512 * (c % 2) : 512 * (c % 2) + 512], in_=y[:]
             )
 
-        xs = []
-        for t in range(4):
-            xs.append(turn_wu(0, t, "S"))
-            quant_wu(0, t, xs[t])
-        for c in range(0, 4):
-            unit(0, c, "S")
-        quant_m(0, 0)
-        for c in range(4, 8):
-            unit(0, c, "S")
-            widen(0, c - 4)
-        quant_m(0, 1)
-        for r in range(4):
-            turn_c(r, "S")
-            widen(1, r)
-        lace(0, 0)
-        lace(1, 0)
-        for c in range(8, 12):
-            unit(0, c, "S")
-        quant_wi(0, 0)
-        quant_c(0)
-        quant_wi(1, 0)
-        quant_c(1)
-        lace(0, 1)
-        ys = []
-        for t in range(4):
-            ys.append(turn_wu(1, t, "S"))
-            quant_wu(1, t, ys[t])
-        lace(1, 1)
-        quant_wi(0, 1)
-        quant_wi(1, 1)
-        for c in range(12, 16):
-            unit(0, c, "S")
-        for t in range(4):
-            hidden(0, t)
-        for c in range(0, 4):
-            unit(1, c, "S")
-        quant_m(0, 2)
-        quant_m(0, 3)
-        gains(0)
-        for t in range(4):
-            hidden(1, t)
-        quant_m(0, 4)
-        quant_h(0)
-        quant_m(0, 5)
-        quant_m(0, 6)
-        for c in range(4, 8):
-            unit(1, c, "SVSV"[c % 4])
-        quant_m(0, 7)
-        gains(1)
-        quant_m(1, 0)
-        quant_m(1, 1)
-        quant_h(1)
-        for c in range(8, 12):
-            unit(1, c, "S")
-        quant_m(1, 2)
-        quant_m(1, 3)
-        for i in range(4):
-            final(i, 0, "VSVS"[i])
-        quant_m(1, 4)
-        quant_m(1, 5)
-        for c in range(12, 16):
-            unit(1, c, "SVSV"[c % 4])
-        quant_m(1, 6)
-        for i in range(4):
-            final(i, 1, "VSVS"[i])
-        quant_m(1, 7)
-        for i in range(4):
-            final(i, 2, "VSVS"[i])
-        for i in range(4):
-            final(i, 3, "VSVS"[i])
+
+        order = (
+            "T00 T01 cT00S q00 T02 cT01S q01 T03 cT02S cT03V q02 q03 w00V U000 w01V U001 cU000S w02V "
+            "U002 cU001S w03V U003 cU002S w10V U004 cU003S w11V U005 cU004S w12V U006 cU005S w13V U007 "
+            "cU006S l00 C0 cU007S C1 cC0S C2 cC1S l10 C3 cC2S T10 cC3S T11 cT10S T12 i00 cT11S T13 i10 "
+            "cT12S U008 k0 cT13S U009 k1 cU008S U010 l01 cU009S U011 cU010S U012 cU011S l11 U013 cU012S "
+            "U014 cU013S U015 cU014S q10 H00 q11 cU015S q12 H01 cH00S q13 H02 i01 cH01S H03 i11 cH02S "
+            "U100 m00 cH03S m01 U101 m02 cU100S g0 U102 cU101S U103 cU102S H10 cU103S H11 cH10S H12 m10 "
+            "cH11S H13 x0 cH12S U104 m11 cH13S m03 U105 m04 cU104S g1 U106 cU105S U107 cU106S U108 "
+            "cU107S U109 cU108S U110 m12 cU109S x1 U111 cU110S m13 Y00 m05 cU111S m14 Y01 m06 cY00S m15 "
+            "Y02 cY01V Y03 m07 cY02S U112 cY03V U113 cU112S U114 cU113V U115 cU114S m16 Y10 cU115V Y11 "
+            "cY10S m17 Y12 cY11S Y13 cY12V Y20 cY13S Y21 cY20V Y22 cY21S Y23 cY22V Y30 cY23S Y31 cY30V "
+            "Y32 cY31S Y33 cY32V cY33S "
+        )
+        for op in order.split():
+            k = op[0]
+            d = [int(x) for x in op[1:] if x in "0123456789"]
+            if k == "T":
+                banks[op] = turn(wu_raw[d[0]][:, d[1], :].bitcast(F32))
+            elif k == "C":
+                banks[op] = turn(craw[:, d[0], :].bitcast(F32))
+            elif k == "U":
+                banks[op] = unit(d[0], 10 * d[1] + d[2])
+            elif k == "H":
+                banks[op] = hidden(d[0], d[1])
+            elif k == "Y":
+                banks[op] = final(d[1], d[0])
+            elif k == "c":
+                eng = op[-1]
+                src = banks[op[1:-1]]
+                k2 = op[1]
+                d = [int(x) for x in op[2:-1]]
+                if k2 == "T":
+                    drain_wu(d[0], d[1], src, eng)
+                elif k2 == "C":
+                    drain_c(d[0], src, eng)
+                elif k2 == "U":
+                    drain_m(d[0], 10 * d[1] + d[2], src, eng)
+                elif k2 == "H":
+                    drain_h(d[0], d[1], src)
+                else:
+                    drain_y(d[1], d[0], src, eng)
+            elif k == "q":
+                quant_wu(d[0], d[1])
+            elif k == "k":
+                quant_c(d[0])
+            elif k == "w":
+                widen(d[0], d[1], op[-1])
+            elif k == "l":
+                lace(d[0], d[1])
+            elif k == "i":
+                quant_wi(d[0], d[1])
+            elif k == "m":
+                quant_m(d[0], d[1])
+            elif k == "g":
+                gains(d[0])
+            else:
+                quant_h(d[0])

@@ -28,7 +28,7 @@ def tile_prefix_tuning_kv_s11_kernel(
         keep = ctx.enter_context(tc.tile_pool(name="keep", bufs=1))
         wst = ctx.enter_context(tc.tile_pool(name="wst", bufs=8))
         mst = ctx.enter_context(tc.tile_pool(name="mst", bufs=16))
-        yst = ctx.enter_context(tc.tile_pool(name="yst", bufs=16))
+        yst = ctx.enter_context(tc.tile_pool(name="yst", bufs=12))
         psum = ctx.enter_context(tc.psum_pool(name="psum", bufs=8))
 
         ident = keep.tile([P, P], F32, name="ident")
@@ -61,6 +61,8 @@ def tile_prefix_tuning_kv_s11_kernel(
 
         ctx.enter_context(tc.manual_schedule())
 
+        zeros = keep.tile([P, 512], BF16, name="zeros", align_bytes=64)
+        nc.vector.memset(zeros[:], 0.0)
         nc.vector.memset(w4s[:, :, 0:512].bitcast(I32), 0)
         nc.vector.memset(w4s[:, :, 512:N].bitcast(I32), 0)
         nc.vector.memset(warm[:], 0.0)
@@ -96,10 +98,10 @@ def tile_prefix_tuning_kv_s11_kernel(
         load_w4(512, 1024)
         load_w4s(512, N)
         nc.sync.dma_start(out=wi[:, 1], in_=wi_src[1])
-        load_w4(1024, N)
         c_src = codes.rearrange("(r p) k -> p r k", p=P)
         for h in range(2):
             nc.sync.dma_start(out=craw[:, 2 * h : 2 * h + 2, :], in_=c_src[:, 2 * h : 2 * h + 2, :])
+        load_w4(1024, N)
         load_wu(1, 0, 2)
         load_wu(1, 2, 4)
         nc.sync.dma_start(out=bcol[:], in_=bias.rearrange("(g p t) -> p g t", p=P, t=4))
@@ -128,6 +130,15 @@ def tile_prefix_tuning_kv_s11_kernel(
             return b
 
         banks = {}
+        dmy = []
+
+        def dummy(n):
+            if not dmy:
+                dmy.append(bank())
+            nc.tensor.matmul(dmy[0][:, 0:n], lhsT=zeros[:, 0:128], rhs=zeros[:, 0:n], start=True, stop=True)
+
+        for i in range(4):
+            dummy(512)
         wux = {}
 
         def drain_wu(g, t, b, eng):
@@ -182,9 +193,8 @@ def tile_prefix_tuning_kv_s11_kernel(
 
         mx_tiles = {}
 
-        def unit(g, c):
-            b = bank()
-            for t in range(4):
+        def unit_part(g, c, b, ts):
+            for t in ts:
                 for a in range(2):
                     nc.tensor.matmul_mx(
                         out=b[:, 128 * t : 128 * t + 128],
@@ -196,6 +206,16 @@ def tile_prefix_tuning_kv_s11_kernel(
                         stop=(a == 1),
                     )
             return b
+
+        def unit(g, c):
+            if g == 0 and c < 4:
+                if c == 0:
+                    for i in range(4):
+                        banks["U00%d" % i] = bank()
+                for i in range(4):
+                    unit_part(0, i, banks["U00%d" % i], [c])
+                return banks["U00%d" % c]
+            return unit_part(g, c, bank(), range(4))
 
         def drain_m(g, c, b, eng):
             if (g, c // 2) not in mx_tiles:
@@ -258,31 +278,37 @@ def tile_prefix_tuning_kv_s11_kernel(
 
         def drain_y(i, c, b, eng):
             y = yst.tile([P, 512], F32, name="y", tag="y", align_bytes=64)
+            dst = (keys if c < 2 else values)[128 * i : 128 * i + 128, 512 * (c % 2) : 512 * (c % 2) + 512]
+            if i == 3 and c == 3:
+                nc.vector.tensor_copy(out=y[:, 0:256], in_=b[:, 0:256])
+                nc.sync.dma_start(out=dst[:, 0:256], in_=y[:, 0:256])
+                nc.scalar.copy(out=y[:, 256:512], in_=b[:, 256:512])
+                nc.scalar.dma_start(out=dst[:, 256:512], in_=y[:, 256:512])
+                return
             copy_out(eng, y[:], b[:])
-            dst = keys if c < 2 else values
-            nc.sync.dma_start(
-                out=dst[128 * i : 128 * i + 128, 512 * (c % 2) : 512 * (c % 2) + 512], in_=y[:]
-            )
+            nc.sync.dma_start(out=dst, in_=y[:])
 
 
         order = (
-            "T00 T01 cT00S q00 T02 cT01S q01 T03 cT02S cT03V q02 q03 w00V U000 w01V U001 cU000S w02V "
-            "U002 cU001S w03V U003 cU002S w10V U004 cU003S w11V U005 cU004S w12V U006 cU005S w13V U007 "
-            "cU006S l00 C0 cU007S C1 cC0S C2 cC1S l10 C3 cC2S T10 cC3S T11 cT10S T12 i00 cT11S T13 i10 "
-            "cT12S U008 k0 cT13S U009 k1 cU008S U010 l01 cU009S U011 cU010S U012 cU011S l11 U013 cU012S "
-            "U014 cU013S U015 cU014S q10 H00 q11 cU015S q12 H01 cH00S q13 H02 i01 cH01S H03 i11 cH02S "
-            "U100 m00 cH03S m01 U101 m02 cU100S g0 U102 cU101S U103 cU102S H10 cU103S H11 cH10S H12 m10 "
-            "cH11S H13 x0 cH12S U104 m11 cH13S m03 U105 m04 cU104S g1 U106 cU105S U107 cU106S U108 "
-            "cU107S U109 cU108S U110 m12 cU109S x1 U111 cU110S m13 Y00 m05 cU111S m14 Y01 m06 cY00S m15 "
-            "Y02 cY01V Y03 m07 cY02S U112 cY03V U113 cU112S U114 cU113V U115 cU114S m16 Y10 cU115V Y11 "
-            "cY10S m17 Y12 cY11S Y13 cY12V Y20 cY13S Y21 cY20V Y22 cY21S Y23 cY22V Y30 cY23S Y31 cY30V "
-            "Y32 cY31S Y33 cY32V cY33S "
+            "T00 T01 cT00S T02 cT01S q00 T03 cT02V U000 q01 cT03S q02 U001 q03 U002 w00V U003 w01V U004 "
+            "cU000S cU001V U005 cU002S cU003V U006 cU004S cU005V U007 cU006S w02V C0 cU007S w03V C1 cC0S "
+            "w10V C2 cC1S w11V C3 cC2S w12V U008 cC3S w13V U009 cU008S l00 U010 cU009S U011 cU010S T10 "
+            "cU011S l10 T11 cT10S T12 cT11S T13 cT12S q10 U012 q11 cT13S i00 U013 cU012S q12 U014 q13 "
+            "cU013S i10 U015 k0 cU014S U100 cU015S k1 U101 l01 cU100S H00 cU101S H01 cH00S H02 cH01S l11 "
+            "H03 cH02S U102 cH03S U103 cU102S i01 U104 cU103S i11 U105 g0 cU104S H10 cU105S H11 cH10S "
+            "H12 cH11S H13 cH12S U106 m00 cH13S x0 U107 cU106S g1 U108 cU107S U109 cU108S U110 cU109S "
+            "U111 cU110S U112 m01 cU111S x1 U113 cU112S m10 U114 m11 cU113S m02 U115 m03 cU114S m12 Y00 "
+            "cU115S m13 Y01 m04 cY00S m05 Y02 m14 cY01S m15 Y03 m06 cY02S m07 Y10 cY03V Y11 m16 cY10S "
+            "m17 Y12 cY11S Y13 cY12V Y20 cY13S Y21 cY20V Y22 cY21S Y23 cY22V Y30 cY23S Y31 cY30V Y32 "
+            "cY31S Y33 cY32V cY33S "
         )
         for op in order.split():
             k = op[0]
             d = [int(x) for x in op[1:] if x in "0123456789"]
             if k == "T":
                 banks[op] = turn(wu_raw[d[0]][:, d[1], :].bitcast(F32))
+                if op in ("T00", "T01", "T02"):
+                    dummy(256)
             elif k == "C":
                 banks[op] = turn(craw[:, d[0], :].bitcast(F32))
             elif k == "U":

@@ -37,8 +37,13 @@ def tile_prefix_tuning_kv_s11_kernel(
         wu_raw = [keep.tile([P, 4, D], BF16, name="wu_raw%d" % g, align_bytes=64) for g in range(2)]
         wuq = [keep.tile([P, 4, 256], U32, name="wuq%d" % g, align_bytes=64) for g in range(2)]
         wus = [keep.tile([P, 4, 256], U8, name="wus%d" % g, align_bytes=64) for g in range(2)]
-        w4 = keep.tile([P, 2, 2 * N], U8, name="w4", align_bytes=64)
-        w4s = keep.tile([P, 2, N], U8, name="w4s", align_bytes=64)
+        cuts = (0, 512, 1024, N)
+        scuts = (0, 512, N)
+        w4, w4s = [], []
+        for i in range(3):
+            w4.append(keep.tile([P, 2, 2 * (cuts[i + 1] - cuts[i])], U8, name="w4_%d" % i, align_bytes=64))
+        for i in range(2):
+            w4s.append(keep.tile([P, 2, scuts[i + 1] - scuts[i]], U8, name="w4s_%d" % i, align_bytes=64))
         craw = keep.tile([P, 4, K], BF16, name="craw", align_bytes=64)
         cg = keep.tile([P, 2, ROWS, 4], BF16, name="cg", align_bytes=64)
         cq = keep.tile([P, 2, ROWS], U32, name="cq", align_bytes=64)
@@ -63,8 +68,8 @@ def tile_prefix_tuning_kv_s11_kernel(
 
         zeros = keep.tile([P, 512], BF16, name="zeros", align_bytes=64)
         nc.vector.memset(zeros[:], 0.0)
-        nc.vector.memset(w4s[:, :, 0:512].bitcast(I32), 0)
-        nc.vector.memset(w4s[:, :, 512:N].bitcast(I32), 0)
+        for i in range(2):
+            nc.vector.memset(w4s[i][:].rearrange("p a n -> p (a n)").bitcast(I32), 0)
         nc.vector.memset(warm[:], 0.0)
         nc.scalar.activation(out=warm[:, 1:2], in_=warm[:, 0:1], func=TANH)
 
@@ -73,35 +78,38 @@ def tile_prefix_tuning_kv_s11_kernel(
         def load_wu(g, t0, t1):
             nc.sync.dma_start(out=wu_raw[g][:, t0:t1, :], in_=wu_src[g][:, t0:t1, :])
 
-        def load_w4(n0, n1):
+        def load_w4(i):
             nc.sync.dma_start(
-                out=w4[:, :, 2 * n0 : 2 * n1].bitcast(I32),
-                in_=wkv_words.rearrange("g p b -> p g b")[:, :, 2 * n0 : 2 * n1].bitcast(I32),
+                out=w4[i][:].bitcast(I32),
+                in_=wkv_words.rearrange("g p b -> p g b")[:, :, 2 * cuts[i] : 2 * cuts[i + 1]].bitcast(I32),
             )
 
-        def load_w4s(n0, n1):
+        def load_w4s(i):
             for q in range(4):
                 nc.sync.dma_start(
-                    out=w4s[32 * q : 32 * q + 4, :, n0:n1].bitcast(I32),
-                    in_=wkv_scales[:, 4 * q : 4 * q + 4, n0:n1].rearrange("g r n -> r g n").bitcast(I32),
+                    out=w4s[i][32 * q : 32 * q + 4, :, :].bitcast(I32),
+                    in_=wkv_scales[:, 4 * q : 4 * q + 4, scuts[i] : scuts[i + 1]]
+                    .rearrange("g r n -> r g n")
+                    .bitcast(I32),
                 )
 
         load_wu(0, 0, 1)
-        load_w4s(0, 512)
+        load_w4s(0)
         load_wu(0, 1, 2)
         load_wu(0, 2, 3)
         load_wu(0, 3, 4)
-        load_w4(0, 512)
+        load_w4(0)
         wi_src = w_in_bytes.rearrange("(g p t) f -> g p t f", p=P, t=4)
         nc.sync.dma_start(out=wisc[:], in_=w_in_scale.rearrange("(g p t) o -> p g (t o)", p=P, t=4))
-        nc.sync.dma_start(out=wi[:, 0], in_=wi_src[0])
-        load_w4(512, 1024)
-        load_w4s(512, N)
+        for h in range(2):
+            nc.sync.dma_start(out=wi[:, 0, 2 * h : 2 * h + 2, :], in_=wi_src[0][:, 2 * h : 2 * h + 2, :])
+        load_w4(1)
+        load_w4s(1)
         nc.sync.dma_start(out=wi[:, 1], in_=wi_src[1])
         c_src = codes.rearrange("(r p) k -> p r k", p=P)
         for h in range(2):
             nc.sync.dma_start(out=craw[:, 2 * h : 2 * h + 2, :], in_=c_src[:, 2 * h : 2 * h + 2, :])
-        load_w4(1024, N)
+        load_w4(2)
         load_wu(1, 0, 2)
         load_wu(1, 2, 4)
         nc.sync.dma_start(out=bcol[:], in_=bias.rearrange("(g p t) -> p g t", p=P, t=4))
@@ -130,15 +138,6 @@ def tile_prefix_tuning_kv_s11_kernel(
             return b
 
         banks = {}
-        dmy = []
-
-        def dummy(n):
-            if not dmy:
-                dmy.append(bank())
-            nc.tensor.matmul(dmy[0][:, 0:n], lhsT=zeros[:, 0:128], rhs=zeros[:, 0:n], start=True, stop=True)
-
-        for i in range(4):
-            dummy(512)
         wux = {}
 
         def drain_wu(g, t, b, eng):
@@ -194,14 +193,18 @@ def tile_prefix_tuning_kv_s11_kernel(
         mx_tiles = {}
 
         def unit_part(g, c, b, ts):
+            i = min(c // 4, 2)
+            n = 128 * c - cuts[i]
+            j = min(c // 4, 1)
+            m = 128 * c - scuts[j]
             for t in ts:
                 for a in range(2):
                     nc.tensor.matmul_mx(
                         out=b[:, 128 * t : 128 * t + 128],
                         lhsT=wuq[g][:, t, 128 * a : 128 * a + 128].bitcast(FP8X4),
                         lhsT_scale=wus[g][:, t, 128 * a : 128 * a + 128],
-                        rhs=w4[:, a, 256 * c : 256 * c + 256].bitcast(FP4X4),
-                        rhs_scale=w4s[:, a, 128 * c : 128 * c + 128],
+                        rhs=w4[i][:, a, 2 * n : 2 * n + 256].bitcast(FP4X4),
+                        rhs_scale=w4s[j][:, a, m : m + 128],
                         start=(a == 0),
                         stop=(a == 1),
                     )
@@ -279,72 +282,90 @@ def tile_prefix_tuning_kv_s11_kernel(
         def drain_y(i, c, b, eng):
             y = yst.tile([P, 512], F32, name="y", tag="y", align_bytes=64)
             dst = (keys if c < 2 else values)[128 * i : 128 * i + 128, 512 * (c % 2) : 512 * (c % 2) + 512]
-            if i == 3 and c == 3:
-                nc.vector.tensor_copy(out=y[:, 0:256], in_=b[:, 0:256])
-                nc.sync.dma_start(out=dst[:, 0:256], in_=y[:, 0:256])
-                nc.scalar.copy(out=y[:, 256:512], in_=b[:, 256:512])
-                nc.scalar.dma_start(out=dst[:, 256:512], in_=y[:, 256:512])
-                return
-            copy_out(eng, y[:], b[:])
-            nc.sync.dma_start(out=dst, in_=y[:])
+            parts = ((0, 512, eng),) if eng in "SV" else ((0, 256, "V"), (256, 512, "S"))
+            for n0, n1, e in parts:
+                copy_out(e, y[:, n0:n1], b[:, n0:n1])
+                nc.sync.dma_start(out=dst[:, n0:n1], in_=y[:, n0:n1])
 
 
-        order = (
-            "T00 T01 cT00S T02 cT01S q00 T03 cT02V U000 q01 cT03S q02 U001 q03 U002 w00V U003 w01V U004 "
-            "cU000S cU001V U005 cU002S cU003V U006 cU004S cU005V U007 cU006S w02V C0 cU007S w03V C1 cC0S "
-            "w10V C2 cC1S w11V C3 cC2S w12V U008 cC3S w13V U009 cU008S l00 U010 cU009S U011 cU010S T10 "
-            "cU011S l10 T11 cT10S T12 cT11S T13 cT12S q10 U012 q11 cT13S i00 U013 cU012S q12 U014 q13 "
-            "cU013S i10 U015 k0 cU014S U100 cU015S k1 U101 l01 cU100S H00 cU101S H01 cH00S H02 cH01S l11 "
-            "H03 cH02S U102 cH03S U103 cU102S i01 U104 cU103S i11 U105 g0 cU104S H10 cU105S H11 cH10S "
-            "H12 cH11S H13 cH12S U106 m00 cH13S x0 U107 cU106S g1 U108 cU107S U109 cU108S U110 cU109S "
-            "U111 cU110S U112 m01 cU111S x1 U113 cU112S m10 U114 m11 cU113S m02 U115 m03 cU114S m12 Y00 "
-            "cU115S m13 Y01 m04 cY00S m05 Y02 m14 cY01S m15 Y03 m06 cY02S m07 Y10 cY03V Y11 m16 cY10S "
-            "m17 Y12 cY11S Y13 cY12V Y20 cY13S Y21 cY20V Y22 cY21S Y23 cY22V Y30 cY23S Y31 cY30V Y32 "
-            "cY31S Y33 cY32V cY33S "
-        )
-        for op in order.split():
-            k = op[0]
-            d = [int(x) for x in op[1:] if x in "0123456789"]
-            if k == "T":
-                banks[op] = turn(wu_raw[d[0]][:, d[1], :].bitcast(F32))
-                if op in ("T00", "T01", "T02"):
-                    dummy(256)
-            elif k == "C":
-                banks[op] = turn(craw[:, d[0], :].bitcast(F32))
-            elif k == "U":
-                banks[op] = unit(d[0], 10 * d[1] + d[2])
-            elif k == "H":
-                banks[op] = hidden(d[0], d[1])
-            elif k == "Y":
-                banks[op] = final(d[1], d[0])
-            elif k == "c":
-                eng = op[-1]
-                src = banks[op[1:-1]]
-                k2 = op[1]
-                d = [int(x) for x in op[2:-1]]
-                if k2 == "T":
-                    drain_wu(d[0], d[1], src, eng)
-                elif k2 == "C":
-                    drain_c(d[0], src, eng)
-                elif k2 == "U":
-                    drain_m(d[0], 10 * d[1] + d[2], src, eng)
-                elif k2 == "H":
-                    drain_h(d[0], d[1], src)
-                else:
-                    drain_y(d[1], d[0], src, eng)
-            elif k == "q":
-                quant_wu(d[0], d[1])
-            elif k == "k":
-                quant_c(d[0])
-            elif k == "w":
-                widen(d[0], d[1], op[-1])
-            elif k == "l":
-                lace(d[0], d[1])
-            elif k == "i":
-                quant_wi(d[0], d[1])
-            elif k == "m":
-                quant_m(d[0], d[1])
-            elif k == "g":
-                gains(d[0])
-            else:
-                quant_h(d[0])
+        def units(g, c0, c1, engs):
+            for c in range(c0, c1):
+                drain_m(g, c, unit_part(g, c, bank(), range(4)), engs[c % len(engs)])
+
+        def hiddens(h):
+            for t in range(4):
+                drain_h(h, t, hidden(h, t))
+
+        def finals(c, engs):
+            for i in range(4):
+                drain_y(i, c, final(i, c), engs[i])
+
+        d = bank()
+        for i in range(3):
+            nc.tensor.matmul(d[:], lhsT=zeros[:, 0:128], rhs=zeros[:], start=True, stop=True)
+
+        for t in range(4):
+            drain_wu(0, t, turn(wu_raw[0][:, t, :].bitcast(F32)), "SSVS"[t])
+            if t > 0:
+                quant_wu(0, t - 1)
+        quant_wu(0, 3)
+        first = []
+        for c in range(4):
+            b = bank()
+            first.append(b)
+        for t in range(4):
+            for c in range(4):
+                unit_part(0, c, first[c], [t])
+        for c in range(4):
+            drain_m(0, c, first[c], "S")
+        for g in range(2):
+            for t in range(4):
+                widen(g, t)
+        units(0, 4, 8, "S")
+        for r in range(4):
+            drain_c(r, turn(craw[:, r, :].bitcast(F32)), "S")
+        for g in range(2):
+            lace(g, 0)
+        for g in range(2):
+            quant_wi(g, 0)
+        for g in range(2):
+            quant_c(g)
+        units(0, 8, 12, "S")
+        for t in range(4):
+            drain_wu(1, t, turn(wu_raw[1][:, t, :].bitcast(F32)), "S")
+        for g in range(2):
+            lace(g, 1)
+        for t in range(4):
+            quant_wu(1, t)
+        for g in range(2):
+            quant_wi(g, 1)
+        units(0, 12, 16, "S")
+        hiddens(0)
+        units(1, 0, 4, "S")
+        hiddens(1)
+        quant_m(0, 0)
+        gains(0)
+        quant_m(0, 1)
+        quant_h(0)
+        quant_m(1, 0)
+        quant_m(1, 1)
+        gains(1)
+        quant_m(0, 2)
+        quant_h(1)
+        units(1, 4, 12, "S")
+        quant_m(0, 3)
+        for d in (2, 3):
+            quant_m(1, d)
+        for g in range(2):
+            for d in (4, 5):
+                quant_m(g, d)
+        finals(0, "SSVS")
+        for d in (6, 7):
+            quant_m(0, d)
+        finals(1, "SVSV")
+        units(1, 12, 14, "SV")
+        quant_m(1, 6)
+        units(1, 14, 16, "SV")
+        quant_m(1, 7)
+        finals(2, "SVSV")
+        finals(3, "SVS2")

from contextlib import ExitStack

import concourse.mybir as mybir
from concourse.masks import make_identity

P = 128
ROWS, K, F, D, N = 512, 1024, 1024, 1024, 2048
FLOPS = 2 * (ROWS * K * F + F * D * N + ROWS * F * N)

F32 = mybir.dt.float32
BF16 = mybir.dt.bfloat16
I32 = mybir.dt.int32
U32 = mybir.dt.uint32
U8 = mybir.dt.uint8
FP8 = mybir.dt.float8_e4m3fn
FP8X4 = mybir.dt.float8_e4m3fn_x4
FP4X4 = mybir.dt.float4_e2m1fn_x4
MULT = mybir.AluOpType.mult
COPY = mybir.ActivationFunctionType.Copy
TANH = mybir.ActivationFunctionType.Tanh


def tile_prefix_tuning_kv_s11_kernel(
    tc, codes, w_in_bytes, w_in_scale, bias, gain, w_up, wkv_words, wkv_scales, keys, values
):
    nc = tc.nc
    with ExitStack() as ctx:
        keep = ctx.enter_context(tc.tile_pool(name="keep", bufs=1))
        wst = ctx.enter_context(tc.tile_pool(name="wst", bufs=8))
        mst = ctx.enter_context(tc.tile_pool(name="mst", bufs=16))
        yst = ctx.enter_context(tc.tile_pool(name="yst", bufs=12))
        psum = ctx.enter_context(tc.psum_pool(name="psum", bufs=8))

        ident = keep.tile([P, P], F32, name="ident")
        make_identity(nc, ident[:])

        wu_raw = [keep.tile([P, 4, D], BF16, name="wu_raw%d" % g, align_bytes=64) for g in range(2)]
        wuq = [keep.tile([P, 4, 256], U32, name="wuq%d" % g, align_bytes=64) for g in range(2)]
        wus = [keep.tile([P, 4, 256], U8, name="wus%d" % g, align_bytes=64) for g in range(2)]
        cuts = (0, 512, 1024, N)
        scuts = (0, 512, N)
        w4, w4s = [], []
        for i in range(3):
            w4.append(keep.tile([P, 2, 2 * (cuts[i + 1] - cuts[i])], U8, name="w4_%d" % i, align_bytes=64))
        for i in range(2):
            w4s.append(keep.tile([P, 2, scuts[i + 1] - scuts[i]], U8, name="w4s_%d" % i, align_bytes=64))
        craw = keep.tile([P, 4, K], BF16, name="craw", align_bytes=64)
        cg = keep.tile([P, 2, ROWS, 4], BF16, name="cg", align_bytes=64)
        cq = keep.tile([P, 2, ROWS], U32, name="cq", align_bytes=64)
        cs = keep.tile([P, 2, ROWS], U8, name="cs", align_bytes=64)
        wi = keep.tile([P, 2, 4, F], U8, name="wi", align_bytes=64)
        wisc = keep.tile([P, 2, 4], F32, name="wisc")
        wb = keep.tile([P, 2, 4, F], BF16, name="wb", align_bytes=64)
        wg = keep.tile([P, 2, 2, 2048], BF16, name="wg", align_bytes=64)
        wq = keep.tile([P, 2, 2, 512], U32, name="wq", align_bytes=64)
        ws = keep.tile([P, 2, 2, 512], U8, name="ws", align_bytes=64)
        bcol = keep.tile([P, 2, 4], BF16, name="bcol")
        gcol = keep.tile([P, 2, 4], BF16, name="gcol")
        th = [keep.tile([P, 4, ROWS], F32, name="th%d" % g, align_bytes=64) for g in range(2)]
        hg = [keep.tile([P, ROWS, 4], BF16, name="hg%d" % g, align_bytes=64) for g in range(2)]
        hq = [keep.tile([P, ROWS], U32, name="hq%d" % g, align_bytes=64) for g in range(2)]
        hs = [keep.tile([P, ROWS], U8, name="hs%d" % g, align_bytes=64) for g in range(2)]
        mq = [keep.tile([P, N], U32, name="mq%d" % g, align_bytes=64) for g in range(2)]
        ms = [keep.tile([P, N], U8, name="ms%d" % g, align_bytes=64) for g in range(2)]
        warm = keep.tile([P, 2], F32, name="warm")

        ctx.enter_context(tc.manual_schedule())

        zeros = keep.tile([P, 512], BF16, name="zeros", align_bytes=64)
        nc.vector.memset(zeros[:], 0.0)
        for i in range(2):
            nc.vector.memset(w4s[i][:].rearrange("p a n -> p (a n)").bitcast(I32), 0)
        nc.vector.memset(warm[:], 0.0)
        nc.scalar.activation(out=warm[:, 1:2], in_=warm[:, 0:1], func=TANH)

        wu_src = w_up.rearrange("(g p t) d -> g p t d", p=P, t=4)

        def load_wu(g, t0, t1):
            nc.sync.dma_start(out=wu_raw[g][:, t0:t1, :], in_=wu_src[g][:, t0:t1, :])

        def load_w4(i):
            nc.sync.dma_start(
                out=w4[i][:].bitcast(I32),
                in_=wkv_words.rearrange("g p b -> p g b")[:, :, 2 * cuts[i] : 2 * cuts[i + 1]].bitcast(I32),
            )

        def load_w4s(i):
            for q in range(4):
                nc.sync.dma_start(
                    out=w4s[i][32 * q : 32 * q + 4, :, :].bitcast(I32),
                    in_=wkv_scales[:, 4 * q : 4 * q + 4, scuts[i] : scuts[i + 1]]
                    .rearrange("g r n -> r g n")
                    .bitcast(I32),
                )

        load_wu(0, 0, 1)
        load_w4s(0)
        load_wu(0, 1, 2)
        load_wu(0, 2, 3)
        load_wu(0, 3, 4)
        load_w4(0)
        wi_src = w_in_bytes.rearrange("(g p t) f -> g p t f", p=P, t=4)
        nc.sync.dma_start(out=wisc[:], in_=w_in_scale.rearrange("(g p t) o -> p g (t o)", p=P, t=4))
        for h in range(2):
            nc.sync.dma_start(out=wi[:, 0, 2 * h : 2 * h + 2, :], in_=wi_src[0][:, 2 * h : 2 * h + 2, :])
        load_w4(1)
        load_w4s(1)
        nc.sync.dma_start(out=wi[:, 1], in_=wi_src[1])
        c_src = codes.rearrange("(r p) k -> p r k", p=P)
        for h in range(2):
            nc.sync.dma_start(out=craw[:, 2 * h : 2 * h + 2, :], in_=c_src[:, 2 * h : 2 * h + 2, :])
        load_w4(2)
        load_wu(1, 0, 2)
        load_wu(1, 2, 4)
        nc.sync.dma_start(out=bcol[:], in_=bias.rearrange("(g p t) -> p g t", p=P, t=4))
        nc.sync.dma_start(out=gcol[:], in_=gain.rearrange("(g p t) -> p g t", p=P, t=4))

        def copy_out(eng, out, in_):
            if eng == "S":
                nc.scalar.copy(out=out, in_=in_)
            else:
                nc.vector.tensor_copy(out=out, in_=in_)

        def bank():
            b = psum.tile([P, 512], F32, name="bank", tag="bank")
            return b

        def turn(words):
            b = bank()
            for a in range(2):
                for u in range(2):
                    i = 2 * a + u
                    nc.tensor.transpose(
                        b[:, 128 * i : 128 * i + 128],
                        words[:, 256 * a + u : 256 * (a + 1) : 2],
                        ident[:],
                    )
            return b

        banks = {}
        wux = {}

        def drain_wu(g, t, b, eng):
            x = wst.tile([P, 2, 128, 4], BF16, name="wux", tag="wux", align_bytes=64)
            wux[(g, t)] = x
            copy_out(eng, x[:].bitcast(F32), b[:].rearrange("p (a u r) -> p a r u", a=2, u=2))

        def quant_wu(g, t):
            x = wux[(g, t)]
            nc.vector.quantize_mx(
                out=wuq[g][:, t, :].bitcast(FP8X4),
                scales=wus[g][:, t, :],
                in_=x[:].rearrange("p a r j -> p (a r j)"),
            )

        def drain_c(r, b, eng):
            copy_out(
                eng,
                cg[:, :, 128 * r : 128 * r + 128, :].bitcast(F32),
                b[:].rearrange("p (a u r) -> p a r u", a=2, u=2),
            )

        def quant_c(g):
            nc.vector.quantize_mx(
                out=cq[:, g, :].bitcast(FP8X4), scales=cs[:, g, :], in_=cg[:, g].rearrange("p n j -> p (n j)")
            )

        def widen(g, t, eng="V"):
            if eng == "S":
                nc.scalar.activation(
                    out=wb[:, g, t, :], in_=wi[:, g, t, :].bitcast(FP8), func=COPY, scale=wisc[:, g, t : t + 1]
                )
                return
            nc.vector.tensor_scalar(
                out=wb[:, g, t, :],
                in0=wi[:, g, t, :].bitcast(FP8),
                scalar1=wisc[:, g, t : t + 1],
                scalar2=None,
                op0=MULT,
            )

        def lace(g, h):
            nc.vector.tensor_copy(
                out=wg[:, g, h, :].rearrange("p (t m j) -> p t m j", t=4, j=4),
                in_=wb[:, g, :, 512 * h : 512 * h + 512].rearrange("p j (m t) -> p t m j", t=4),
            )

        def quant_wi(g, h):
            nc.vector.quantize_mx(
                out=wq[:, g, h, :].bitcast(FP8X4), scales=ws[:, g, h, :], in_=wg[:, g, h, :]
            )

        mx_tiles = {}

        def unit_part(g, c, b, ts):
            i = min(c // 4, 2)
            n = 128 * c - cuts[i]
            j = min(c // 4, 1)
            m = 128 * c - scuts[j]
            for t in ts:
                for a in range(2):
                    nc.tensor.matmul_mx(
                        out=b[:, 128 * t : 128 * t + 128],
                        lhsT=wuq[g][:, t, 128 * a : 128 * a + 128].bitcast(FP8X4),
                        lhsT_scale=wus[g][:, t, 128 * a : 128 * a + 128],
                        rhs=w4[i][:, a, 2 * n : 2 * n + 256].bitcast(FP4X4),
                        rhs_scale=w4s[j][:, a, m : m + 128],
                        start=(a == 0),
                        stop=(a == 1),
                    )
            return b

        def unit(g, c):
            if g == 0 and c < 4:
                if c == 0:
                    for i in range(4):
                        banks["U00%d" % i] = bank()
                for i in range(4):
                    unit_part(0, i, banks["U00%d" % i], [c])
                return banks["U00%d" % c]
            return unit_part(g, c, bank(), range(4))

        def drain_m(g, c, b, eng):
            if (g, c // 2) not in mx_tiles:
                x = mst.tile([P, 2, 128, 4], BF16, name="mx", tag="mx", align_bytes=64)
                mx_tiles[(g, c // 2)] = x
            x = mx_tiles[(g, c // 2)]
            copy_out(eng, x[:, c % 2], b[:].rearrange("p (t n) -> p n t", t=4))

        def quant_m(g, d):
            x = mx_tiles[(g, d)]
            nc.vector.quantize_mx(
                out=mq[g][:, 256 * d : 256 * d + 256].bitcast(FP8X4),
                scales=ms[g][:, 256 * d : 256 * d + 256],
                in_=x[:].rearrange("p i n j -> p (i n j)"),
            )

        def hidden(h, t):
            b = bank()
            for g in range(2):
                nc.tensor.matmul_mx(
                    out=b[:],
                    lhsT=wq[:, g, h, 128 * t : 128 * t + 128].bitcast(FP8X4),
                    lhsT_scale=ws[:, g, h, 128 * t : 128 * t + 128],
                    rhs=cq[:, g, :].bitcast(FP8X4),
                    rhs_scale=cs[:, g, :],
                    start=(g == 0),
                    stop=(g == 1),
                )
            return b

        def drain_h(h, t, b):
            nc.scalar.activation(out=th[h][:, t, :], in_=b[:], func=TANH, bias=bcol[:, h, t : t + 1])

        def gains(h):
            nc.vector.tensor_tensor(
                out=hg[h][:],
                in0=th[h][:].rearrange("p t n -> p n t"),
                in1=gcol[:, h, :].unsqueeze(1).to_broadcast([P, ROWS, 4]),
                op=MULT,
            )

        def quant_h(h):
            nc.vector.quantize_mx(
                out=hq[h][:].bitcast(FP8X4), scales=hs[h][:], in_=hg[h][:].rearrange("p n j -> p (n j)")
            )

        def final(i, c):
            b = bank()
            for g in range(2):
                nc.tensor.matmul_mx(
                    out=b[:],
                    lhsT=hq[g][:, 128 * i : 128 * i + 128].bitcast(FP8X4),
                    lhsT_scale=hs[g][:, 128 * i : 128 * i + 128],
                    rhs=mq[g][:, 512 * c : 512 * c + 512].bitcast(FP8X4),
                    rhs_scale=ms[g][:, 512 * c : 512 * c + 512],
                    start=(g == 0),
                    stop=(g == 1),
                )
            return b

        def drain_y(i, c, b, eng):
            y = yst.tile([P, 512], F32, name="y", tag="y", align_bytes=64)
            dst = (keys if c < 2 else values)[128 * i : 128 * i + 128, 512 * (c % 2) : 512 * (c % 2) + 512]
            parts = ((0, 512, eng),) if eng in "SV" else ((0, 256, "V"), (256, 512, "S"))
            for n0, n1, e in parts:
                copy_out(e, y[:, n0:n1], b[:, n0:n1])
                nc.sync.dma_start(out=dst[:, n0:n1], in_=y[:, n0:n1])


        def units(g, c0, c1, engs):
            for c in range(c0, c1):
                drain_m(g, c, unit_part(g, c, bank(), range(4)), engs[c % len(engs)])

        def hiddens(h):
            for t in range(4):
                drain_h(h, t, hidden(h, t))

        def finals(c, engs):
            for i in range(4):
                drain_y(i, c, final(i, c), engs[i])

        d = bank()
        for i in range(3):
            nc.tensor.matmul(d[:], lhsT=zeros[:, 0:128], rhs=zeros[:], start=True, stop=True)

        for t in range(4):
            drain_wu(0, t, turn(wu_raw[0][:, t, :].bitcast(F32)), "SSVS"[t])
            if t > 0:
                quant_wu(0, t - 1)
        quant_wu(0, 3)
        first = []
        for c in range(4):
            b = bank()
            first.append(b)
        for t in range(4):
            for c in range(4):
                unit_part(0, c, first[c], [t])
        for c in range(4):
            drain_m(0, c, first[c], "S")
        for g in range(2):
            for t in range(4):
                widen(g, t)
        units(0, 4, 8, "S")
        for r in range(4):
            drain_c(r, turn(craw[:, r, :].bitcast(F32)), "S")
        for g in range(2):
            lace(g, 0)
        for g in range(2):
            quant_wi(g, 0)
        for g in range(2):
            quant_c(g)
        units(0, 8, 12, "S")
        for t in range(4):
            drain_wu(1, t, turn(wu_raw[1][:, t, :].bitcast(F32)), "S")
        for g in range(2):
            lace(g, 1)
        for t in range(4):
            quant_wu(1, t)
        for g in range(2):
            quant_wi(g, 1)
        units(0, 12, 16, "S")
        hiddens(0)
        units(1, 0, 4, "S")
        hiddens(1)
        quant_m(0, 0)
        gains(0)
        quant_m(0, 1)
        quant_h(0)
        quant_m(1, 0)
        quant_m(1, 1)
        gains(1)
        quant_m(0, 2)
        quant_h(1)
        units(1, 4, 12, "S")
        quant_m(0, 3)
        for d in (2, 3):
            quant_m(1, d)
        for g in range(2):
            for d in (4, 5):
                quant_m(g, d)
        finals(0, "SSVS")
        for d in (6, 7):
            quant_m(0, d)
        finals(1, "SVSV")
        units(1, 12, 14, "SV")
        quant_m(1, 6)
        units(1, 14, 16, "SV")
        quant_m(1, 7)
        finals(2, "SVSV")
        finals(3, "SVS2")
